import numpy as np
import ml_dtypes


def mxq(x, axis, fmt="e4m3"):
    dtype, down = {"e4m3": (ml_dtypes.float8_e4m3fn, 7), "e5m2": (ml_dtypes.float8_e5m2, 14)}[fmt]
    v = np.moveaxis(np.asarray(x, np.float32).astype(ml_dtypes.bfloat16).astype(np.float64), axis, -1)
    blocks = v.reshape(v.shape[:-1] + (-1, 32))
    amax = np.abs(blocks).max(-1, keepdims=True)
    byte = np.maximum(np.where(amax > 0, np.frexp(amax)[1] - 1 + 127, 0) - down, 1)
    scale = np.exp2(byte - 127.0)
    codes = (blocks / scale).astype(np.float32).astype(dtype).astype(np.float64)
    return np.moveaxis((codes * scale).reshape(v.shape), -1, axis)


WIDE = False


def mx_kscale(k):
    if not WIDE:
        return np.ones(k)
    levels = np.array([10, -10, 5, -5, 0])
    if k % 512:
        return np.exp2(np.random.permutation(np.resize(levels, k // 32))).repeat(32)
    a = np.empty((k // 512, 16))
    for p in range(k // 512):
        a[p, :8] = np.random.permutation(np.resize(levels, 8))
        for g in range(8):
            far = levels[np.abs(levels - a[p, g]) >= 10]
            a[p, g + 8] = far[np.random.randint(len(far))]
    return np.exp2(a.ravel()).repeat(32)


BF16 = ml_dtypes.bfloat16


def bf(x):
    return np.asarray(x, np.float32).astype(BF16)


def f64(x):
    return np.asarray(x).astype(np.float64)


E2M1 = np.array([0.0, 0.5, 1.0, 1.5, 2.0, 3.0, 4.0, 6.0, -0.0, -0.5, -1.0, -1.5, -2.0, -3.0, -4.0, -6.0])


def pack_weight(w, fmt):
    k, n = w.shape
    w = f64(bf(w)).reshape(k // 32, 32, n)
    amax = np.abs(w).max(1)
    if fmt == "e4m3":
        byte = np.frexp(amax)[1] - 1 + 127 - 7
    else:
        mant, ex = np.frexp(amax / 6.0)
        byte = np.where(mant > 0.5, ex, ex - 1) + 127
    byte = np.clip(np.where(amax > 0, byte, 1), 1, 254)
    scaled = (w * np.exp2(127.0 - byte)[:, None, :]).reshape(k, n).astype(np.float32)
    by_word = np.ascontiguousarray(scaled.reshape(k // 512, 128, 4, n).transpose(0, 1, 3, 2))
    if fmt == "e4m3":
        words = by_word.astype(ml_dtypes.float8_e4m3fn).view(np.uint8)
    else:
        c = by_word.astype(ml_dtypes.float4_e2m1fn).view(np.uint8) & 0xF
        words = c[..., 0::2] | (c[..., 1::2] << 4)
    return np.ascontiguousarray(words), np.ascontiguousarray(byte.astype(np.uint8).reshape(k // 512, 16, n))


def unpack_weight(words, scales, fmt):
    g, p, n, _ = words.shape
    if fmt == "e4m3":
        vals = np.ascontiguousarray(words).view(ml_dtypes.float8_e4m3fn).astype(np.float64)
    else:
        nib = np.empty((g, p, n, 4), np.uint8)
        nib[..., 0::2] = words & 0xF
        nib[..., 1::2] = words >> 4
        vals = E2M1[nib]
    vals = vals * np.repeat(np.exp2(scales.astype(np.float64) - 127.0), 8, axis=1)[..., None]
    return vals.transpose(0, 1, 3, 2).reshape(g * 512, n)
def pack4(w):
    words, scales = pack_weight(w, "e2m1")
    return words.reshape(words.shape[0], 128, -1), scales


def unpack4(words, scales):
    return unpack_weight(words.reshape(words.shape[0], 128, -1, 2), scales, "e2m1")


P, D, F, R, N, B = 2048, 1024, 1024, 512, 1024, 8


def setup_inputs():
    s = mx_kscale(D)
    c = mx_kscale(F)
    r = mx_kscale(R)
    root = F ** 0.25
    x = np.random.standard_normal((P, D)) * s
    w = np.random.standard_normal((D, F)) / np.sqrt(D) / root / s[:, None] * c
    u = np.random.standard_normal((R, F)) * r[:, None] / c
    v = np.random.standard_normal((R, N)) / np.sqrt(R) / root / r[:, None]
    u_words, u_scales = pack4(u)
    v_words, v_scales = pack4(v)
    return {"x": bf(x), "w": bf(w),
            "u_words": u_words, "u_scales": u_scales,
            "v_words": v_words, "v_scales": v_scales}


def reference(x, w, u_words, u_scales, v_words, v_scales):
    h = np.maximum(mxq(f64(x), 1, "e4m3") @ mxq(f64(w), 0, "e4m3"), 0.0)
    e = unpack4(u_words, u_scales).T @ unpack4(v_words, v_scales)
    y = np.maximum(mxq(h, 1, "e4m3") @ mxq(e, 0, "e4m3"), 0.0)
    return y.reshape(P // B, B, N).max(axis=1)

@@ -1,0 +1,376 @@
+from contextlib import ExitStack
+
+import concourse.mybir as mybir
+from concourse.masks import make_identity
+
+FLOPS = 2 * 2048 * 1024 * 1024 * 2 + 2 * 512 * 1024 * 1024
+
+F32 = mybir.dt.float32
+BF16 = mybir.dt.bfloat16
+I32 = mybir.dt.int32
+U32 = mybir.dt.uint32
+U8 = mybir.dt.uint8
+FP8X4 = mybir.dt.float8_e4m3fn_x4
+FP4X4 = mybir.dt.float4_e2m1fn_x4
+MAX = mybir.AluOpType.max
+RELU = mybir.ActivationFunctionType.Relu
+
+REORDERED = (2, 3)
+
+
+def tile_pointnet_set_encoder_s12_kernel(tc, x, w, u_words, u_scales, v_words, v_scales, out):
+    nc = tc.nc
+    with ExitStack() as ctx:
+        keep = ctx.enter_context(tc.tile_pool(name="keep", bufs=1))
+        psum = ctx.enter_context(tc.psum_pool(name="psum", bufs=1))
+        ctx.enter_context(tc.manual_schedule())
+
+        def sb(shape, dtype, tag, bufs=1):
+            t = keep.tile(shape, dtype, name=tag, tag=tag, bufs=bufs, align_bytes=256)
+            return t
+
+        def bank(shape, tag):
+            t = psum.tile(shape, F32, name=tag, tag=tag, bufs={"h": 3, "y": 3, "tr": 2}[tag])
+            return t
+
+        u_raw = sb([128, 2048], U8, "u_raw")
+        u_w = sb([128, 2048], U8, "u_w")
+        u_pl_raw = sb([128, 1024], U8, "u_pl_raw")
+        u_pl = sb([128, 1024], U8, "u_pl")
+        v_lo = sb([128, 1024], U8, "v_lo")
+        v_hi = sb([128, 1024], U8, "v_hi")
+        v_w = sb([128, 1024], U8, "v_w")
+        v_pl = sb([128, 1024], U8, "v_pl")
+        ident = sb([128, 128], F32, "ident")
+        zero = sb([128, 512], BF16, "zero")
+        junk = sb([128, 16], BF16, "junk")
+        x_sb = [sb([128, 4096], BF16, "x_sb%d" % c) for c in range(4)]
+        w_raw = {(g, G): sb([128, 4, 512], BF16, "w_raw%d%d" % (g, G)) for G in range(2) for g in range(2)}
+        w_c = {(g, G): sb([128, 512], U32, "w_c%d%d" % (g, G)) for G in range(2) for g in range(2)}
+        w_s = {(g, G): sb([128, 512], U8, "w_s%d%d" % (g, G)) for G in range(2) for g in range(2)}
+        e_c = {(G, h): sb([128, 512], U32, "e_c%d%d" % (G, h)) for G in range(2) for h in range(2)}
+        e_s = {(G, h): sb([128, 512], U8, "e_s%d%d" % (G, h)) for G in range(2) for h in range(2)}
+        h_c = {(c, G): sb([128, 512], U32, "h_c%d%d" % (c, G)) for c in range(4) for G in range(2)}
+        h_s = {(c, G): sb([128, 512], U8, "h_s%d%d" % (c, G)) for c in range(4) for G in range(2)}
+        acc = [sb([128, 1024], F32, "acc%d" % s) for s in range(2)]
+
+        nc.vector.memset(zero[:], 0.0)
+        nc.vector.memset(u_pl_raw[:].bitcast(I32), 0)
+        nc.vector.memset(v_pl[:].bitcast(I32), 0)
+        make_identity(nc, ident[:])
+        nc.gpsimd.memset(v_lo[64:128, :].bitcast(I32), 0)
+        nc.gpsimd.memset(v_hi[0:64, :].bitcast(I32), 0)
+
+        v32 = v_words[0].bitcast(I32)
+        us32 = u_scales[0].bitcast(I32)
+        vs32 = v_scales[0].bitcast(I32)
+
+        xv = x.rearrange("(s i b) k -> s i b k", s=2, i=128, b=8)
+        wv = w.rearrange("(g p j) f -> g p j f", g=2, p=128, j=4)
+
+        def load_x(c, b0, nb):
+            s, base = c // 2, 4 * (c % 2)
+            nc.sync.dma_start(
+                out=x_sb[c][:].rearrange("p (b k) -> p b k", b=4)[:, b0 : b0 + nb, :],
+                in_=xv[s][:, base + b0 : base + b0 + nb, :],
+            )
+
+        def load_w(g, G):
+            nc.sync.dma_start(out=w_raw[g, G][:], in_=wv[g][:, :, 512 * G : 512 * G + 512])
+
+        load_w(0, 0)
+        load_x(0, 0, 2)
+        load_w(1, 0)
+        load_x(0, 2, 2)
+        for Q in range(4):
+            nc.scalar.dma_start(out=u_pl_raw[32 * Q : 32 * Q + 4, :].bitcast(I32), in_=us32[4 * Q : 4 * Q + 4, :])
+        nc.sync.dma_start(out=u_raw[:].bitcast(I32), in_=u_words[0].bitcast(I32))
+        nc.sync.dma_start(out=v_lo[0:64, :].bitcast(I32), in_=v32[0:64, 0:256])
+        nc.sync.dma_start(out=v_hi[64:128, :].bitcast(I32), in_=v32[64:128, 0:256])
+        for Q in range(4):
+            nc.sync.dma_start(out=v_pl[32 * Q : 32 * Q + 4, :].bitcast(I32), in_=vs32[4 * Q : 4 * Q + 4, :])
+        load_w(0, 1)
+        load_w(1, 1)
+        load_x(1, 0, 4)
+        nc.sync.dma_start(out=v_w[:].bitcast(I32), in_=v32[:, 256:512])
+        load_x(2, 0, 4)
+        load_x(3, 0, 4)
+        nc.scalar.activation(out=junk[:, 0:1], in_=zero[:, 0:1], func=RELU)
+
+        warm = bank([128, 512], "y")
+
+        def spin(n):
+            for i in range(n):
+                nc.tensor.matmul(warm[:], lhsT=zero[:, 0:128], rhs=zero[:], start=True, stop=True)
+
+        spin(6)
+
+        def permute_u(G):
+            nc.vector.tensor_copy(
+                out=u_w[:].bitcast(I32).rearrange("p (G t q r) -> p G t q r", G=2, t=4, q=16, r=4)[:, G],
+                in_=u_raw[:].bitcast(I32).rearrange("p (G q t r) -> p G t q r", G=2, q=16, t=4, r=4)[:, G],
+            )
+
+        def permute_u_scales(G):
+            nc.vector.tensor_copy(
+                out=u_pl[:].bitcast(I32).rearrange("p (G t q r) -> p G t q r", G=2, t=4, q=16, r=2)[:, G],
+                in_=u_pl_raw[:].bitcast(I32).rearrange("p (G q t r) -> p G t q r", G=2, q=16, t=4, r=2)[:, G],
+            )
+
+        def copy(engine, out, in_):
+            if engine == "S":
+                nc.scalar.copy(out, in_)
+            else:
+                nc.vector.tensor_copy(out=out, in_=in_)
+
+        e_grp = {}
+        e_tmp = {}
+        e_bank = {}
+
+        def u_tile(G, t):
+            c0 = G * 512 + t * 128
+            return u_w[:, 2 * c0 : 2 * c0 + 256].bitcast(FP4X4), u_pl[:, c0 : c0 + 128]
+
+        def e0_mm(G, nq, tag):
+            if nq == 0:
+                e_grp[G, 0] = sb([128, 2048], BF16, "e_grp", 2)
+            e = bank([128, 4, 128], tag)
+            n = slice(nq * 128, nq * 128 + 128)
+            for t in range(4):
+                lhsT, lhsT_scale = u_tile(G, t)
+                for part, v in enumerate((v_lo, v_hi)):
+                    nc.tensor.matmul_mx(
+                        out=e[:, t, :], lhsT=lhsT, lhsT_scale=lhsT_scale,
+                        rhs=v[:, 2 * nq * 128 : 2 * nq * 128 + 256].bitcast(FP4X4), rhs_scale=v_pl[:, n],
+                        start=part == 0, stop=part == 1,
+                    )
+            e_bank[G, nq] = e
+
+        def e0_out(G, nq, engine):
+            copy(
+                engine,
+                e_grp[G, 0][:, 512 * nq : 512 * nq + 512].rearrange("p (n t) -> p n t", t=4),
+                e_bank[G, nq][:].rearrange("p t n -> p n t"),
+            )
+
+        def e1_mm(G, t, tag):
+            if t == 0:
+                e_tmp[G] = sb([128, 4, 512], BF16, "e_tmp", 2)
+            e = bank([128, 512], tag)
+            lhsT, lhsT_scale = u_tile(G, t)
+            nc.tensor.matmul_mx(
+                out=e[:], lhsT=lhsT, lhsT_scale=lhsT_scale,
+                rhs=v_w[:].bitcast(FP4X4), rhs_scale=v_pl[:, 512:1024], start=True, stop=True,
+            )
+            e_bank[G, 4 + t] = e
+
+        def e1_out(G, t, engine):
+            copy(engine, e_tmp[G][:, t, :], e_bank[G, 4 + t][:])
+
+        def e1_weave(G):
+            e_grp[G, 1] = sb([128, 2048], BF16, "e_grp", 2)
+            nc.vector.tensor_copy(
+                out=e_grp[G, 1][:].rearrange("p (n t) -> p n t", t=4), in_=e_tmp[G][:].rearrange("p t n -> p n t")
+            )
+
+        def e_quant(G, h):
+            nc.vector.quantize_mx(out=e_c[G, h][:].bitcast(FP8X4), scales=e_s[G, h][:], in_=e_grp[G, h][:])
+
+        x_r = {}
+        x_g = {}
+        x_c = {}
+        x_s = {}
+        x_bank = {}
+
+        def x_reorder(c, bp):
+            if bp == 0:
+                x_r[c] = sb([128, 4096], BF16, "x_r", 2)
+            half = slice(1024 * bp, 1024 * bp + 1024)
+            nc.vector.tensor_copy(
+                out=x_r[c][:].bitcast(F32)[:, half].rearrange("p (a u w) -> p a u w", u=2, w=128),
+                in_=x_sb[c][:].bitcast(F32)[:, half].rearrange("p (a w u) -> p a u w", u=2, w=128),
+            )
+
+        def x_transpose(c, bp, g, tag):
+            if (bp, g) == (0, 0):
+                x_g[c] = sb([128, 4096], BF16, "x_g", 2)
+                x_c[c] = sb([128, 1024], U32, "x_c", 2)
+                x_s[c] = sb([128, 1024], U8, "x_s", 2)
+            xt = bank([128, 2, 256], tag)
+            for u in range(2):
+                for bb in range(2):
+                    base = (2 * bp + bb) * 512 + g * 256
+                    if c in REORDERED:
+                        words = x_r[c][:].bitcast(F32)[:, base + 128 * u : base + 128 * u + 128]
+                    else:
+                        words = x_sb[c][:].bitcast(F32)[:, base + u : base + 256 : 2]
+                    nc.tensor.transpose(xt[:, u, 128 * bb : 128 * bb + 128], words, ident[:])
+            x_bank[c, bp, g] = xt
+
+        def x_out(c, bp, g, engine):
+            base = (2 * bp + g) * 1024
+            copy(
+                engine,
+                x_g[c][:, base : base + 1024].bitcast(F32).rearrange("p (n u) -> p n u", u=2),
+                x_bank[c, bp, g][:].rearrange("p u n -> p n u"),
+            )
+
+        def x_quant(c, bp):
+            nc.vector.quantize_mx(
+                out=x_c[c][:, 512 * bp : 512 * bp + 512].bitcast(FP8X4),
+                scales=x_s[c][:, 512 * bp : 512 * bp + 512],
+                in_=x_g[c][:, 2048 * bp : 2048 * bp + 2048],
+            )
+
+        w_grp = {}
+
+        def w_weave(g, G, engine, ts=(0, 1, 2, 3)):
+            if ts[0] == 0:
+                w_grp[g, G] = sb([128, 2048], BF16, "w_grp", 4)
+            dst = w_grp[g, G][:].rearrange("p (t q r j) -> p t q r j", t=4, q=16, r=8, j=4)
+            src = w_raw[g, G][:].rearrange("p j (q t r) -> p t q r j", q=16, t=4, r=8)
+            if engine == "V":
+                nc.vector.tensor_copy(out=dst[:, ts[0] : ts[-1] + 1], in_=src[:, ts[0] : ts[-1] + 1])
+            else:
+                for t in ts:
+                    nc.scalar.copy(dst[:, t], src[:, t])
+
+        def w_quant(g, G):
+            nc.vector.quantize_mx(out=w_c[g, G][:].bitcast(FP8X4), scales=w_s[g, G][:], in_=w_grp[g, G][:])
+
+        h_t = {}
+        h_bank = {}
+
+        def mm1(c, i):
+            G, b = i // 4, i % 4
+            if b == 0:
+                h_t[c, G] = sb([128, 2048], BF16, "h_t", 3)
+            h = bank([128, 4, 128], "h")
+            col = (b // 2) * 512 + (b % 2) * 128
+            for t in range(4):
+                for g in range(2):
+                    k = slice(col + 256 * g, col + 256 * g + 128)
+                    nc.tensor.matmul_mx(
+                        out=h[:, t, :],
+                        lhsT=w_c[g, G][:, 128 * t : 128 * t + 128].bitcast(FP8X4),
+                        lhsT_scale=w_s[g, G][:, 128 * t : 128 * t + 128],
+                        rhs=x_c[c][:, k].bitcast(FP8X4), rhs_scale=x_s[c][:, k],
+                        start=g == 0, stop=g == 1,
+                    )
+            nc.scalar.activation(
+                out=h_t[c, G][:, 512 * b : 512 * b + 512].rearrange("p (n t) -> p n t", t=4),
+                in_=h[:].rearrange("p t n -> p n t"), func=RELU,
+            )
+
+        def h_quant(c, G):
+            nc.vector.quantize_mx(out=h_c[c, G][:].bitcast(FP8X4), scales=h_s[c, G][:], in_=h_t[c, G][:])
+
+        def mm2(c, b, nh):
+            y = bank([128, 512], "y")
+            rows = slice(128 * b, 128 * b + 128)
+            for G in range(2):
+                nc.tensor.matmul_mx(
+                    out=y[:],
+                    lhsT=h_c[c, G][:, rows].bitcast(FP8X4), lhsT_scale=h_s[c, G][:, rows],
+                    rhs=e_c[G, nh][:].bitcast(FP8X4), rhs_scale=e_s[G, nh][:],
+                    start=G == 0, stop=G == 1,
+                )
+            a = acc[c // 2][:, 512 * nh : 512 * nh + 512]
+            if c % 2 == 0 and b == 0:
+                nc.scalar.activation(out=a, in_=y[:], func=RELU)
+            else:
+                nc.vector.tensor_tensor(out=a, in0=y[:], in1=a, op=MAX)
+            if c % 2 == 1 and b == 3:
+                s = c // 2
+                nc.sync.dma_start(out=out[128 * s : 128 * s + 128, 512 * nh : 512 * nh + 512], in_=a)
+
+        w_weave(0, 0, "S", (0, 1))
+        w_weave(0, 0, "V", (2, 3))
+        for g in range(2):
+            x_transpose(0, 0, g, "tr")
+            x_out(0, 0, g, "S")
+        spin(2)
+        w_quant(0, 0)
+        w_weave(1, 0, "V")
+        w_quant(1, 0)
+        x_quant(0, 0)
+        for g in range(2):
+            x_transpose(0, 1, g, "h")
+            x_out(0, 1, g, "S")
+        spin(2)
+        x_quant(0, 1)
+
+        mm1(0, 0)
+        permute_u(0)
+        permute_u_scales(0)
+        mm1(0, 1)
+        permute_u(1)
+        permute_u_scales(1)
+        mm1(0, 2)
+        mm1(0, 3)
+        w_weave(0, 1, "V")
+        for nq in range(4):
+            e0_mm(0, nq, "y" if nq < 2 else "tr")
+            e0_out(0, nq, "S")
+        w_quant(0, 1)
+        w_weave(1, 1, "V")
+        w_quant(1, 1)
+        for g in range(2):
+            x_transpose(1, 0, g, "tr")
+            x_out(1, 0, g, "S")
+        for nq in range(4):
+            e0_mm(1, nq, "y")
+            e0_out(1, nq, "VS"[nq % 2])
+        h_quant(0, 0)
+        mm1(0, 4)
+        x_quant(1, 0)
+        e_quant(0, 0)
+        mm1(0, 5)
+        for g in range(2):
+            x_transpose(1, 1, g, "tr")
+            x_out(1, 1, g, "V")
+        mm1(0, 6)
+        e_quant(1, 0)
+        x_quant(1, 1)
+        mm1(0, 7)
+
+        second = [(0, b, 0) for b in range(4)] + [(0, b, 1) for b in range(4)]
+        second += [(c, b, nh) for c in (1, 2, 3) for b in range(4) for nh in range(2)]
+        e1_slots = {0: (0, (0, 1)), 1: (0, (2, 3)), 4: (1, (0, 1)), 5: (1, (2, 3))}
+        done = 0
+        for c in (1, 2, 3):
+            for i in range(8):
+                mm1(c, i)
+                if i == 1:
+                    h_quant(c - 1, 1)
+                if i == 4 and c < 3:
+                    x_quant(c + 1, 0)
+                if i == 5:
+                    h_quant(c, 0)
+                if i == 7 and c < 3:
+                    x_quant(c + 1, 1)
+                if c < 3 and i in (0, 3):
+                    x_reorder(c + 1, i // 3)
+                if c == 1 and i in e1_slots:
+                    G, ts = e1_slots[i]
+                    for t in ts:
+                        e1_mm(G, t, "y")
+                        e1_out(G, t, "SV"[t % 2])
+                    if ts[1] == 3:
+                        e1_weave(G)
+                else:
+                    mm2(*second[done])
+                    done += 1
+                if c == 1 and i == 3:
+                    e_quant(0, 1)
+                if c == 1 and i == 7:
+                    e_quant(1, 1)
+                if c < 3 and i in (2, 5):
+                    bp = i // 3
+                    for g in range(2):
+                        x_transpose(c + 1, bp, g, "tr")
+                    for g in range(2):
+                        x_out(c + 1, bp, g, "S")
+        h_quant(3, 1)
+        for item in second[done:]:
+            mm2(*item)

@@ -29,17 +29,15 @@ def tile_pointnet_set_encoder_s12_kernel(tc, x, w, u_words, u_scales, v_words, v
             t = keep.tile(shape, dtype, name=tag, tag=tag, bufs=bufs, align_bytes=256)
             return t
 
-        def bank(shape, tag):
-            t = psum.tile(shape, F32, name=tag, tag=tag, bufs={"h": 3, "y": 3, "tr": 2}[tag])
+        def bank(shape):
+            t = psum.tile(shape, F32, name="bank", tag="bank", bufs=8)
             return t
 
         u_raw = sb([128, 2048], U8, "u_raw")
         u_w = sb([128, 2048], U8, "u_w")
         u_pl_raw = sb([128, 1024], U8, "u_pl_raw")
         u_pl = sb([128, 1024], U8, "u_pl")
-        v_lo = sb([128, 1024], U8, "v_lo")
-        v_hi = sb([128, 1024], U8, "v_hi")
-        v_w = sb([128, 1024], U8, "v_w")
+        v_w = sb([128, 2048], U8, "v_w")
         v_pl = sb([128, 1024], U8, "v_pl")
         ident = sb([128, 128], F32, "ident")
         zero = sb([128, 512], BF16, "zero")
@@ -57,9 +55,6 @@ def tile_pointnet_set_encoder_s12_kernel(tc, x, w, u_words, u_scales, v_words, v
         nc.vector.memset(zero[:], 0.0)
         nc.vector.memset(u_pl_raw[:].bitcast(I32), 0)
         nc.vector.memset(v_pl[:].bitcast(I32), 0)
-        make_identity(nc, ident[:])
-        nc.gpsimd.memset(v_lo[64:128, :].bitcast(I32), 0)
-        nc.gpsimd.memset(v_hi[0:64, :].bitcast(I32), 0)
 
         v32 = v_words[0].bitcast(I32)
         us32 = u_scales[0].bitcast(I32)
@@ -78,32 +73,32 @@ def tile_pointnet_set_encoder_s12_kernel(tc, x, w, u_words, u_scales, v_words, v
         def load_w(g, G):
             nc.sync.dma_start(out=w_raw[g, G][:], in_=wv[g][:, :, 512 * G : 512 * G + 512])
 
-        load_w(0, 0)
+        make_identity(nc, ident[:])
+        for Q in range(3):
+            nc.gpsimd.dma_start(out=v_pl[32 * Q : 32 * Q + 4, :].bitcast(I32), in_=vs32[4 * Q : 4 * Q + 4, :])
         load_x(0, 0, 2)
-        load_w(1, 0)
-        load_x(0, 2, 2)
+        nc.sync.dma_start(out=u_raw[:].bitcast(I32), in_=u_words[0].bitcast(I32))
+        nc.sync.dma_start(out=v_w[:].bitcast(I32), in_=v32)
         for Q in range(4):
             nc.scalar.dma_start(out=u_pl_raw[32 * Q : 32 * Q + 4, :].bitcast(I32), in_=us32[4 * Q : 4 * Q + 4, :])
-        nc.sync.dma_start(out=u_raw[:].bitcast(I32), in_=u_words[0].bitcast(I32))
-        nc.sync.dma_start(out=v_lo[0:64, :].bitcast(I32), in_=v32[0:64, 0:256])
-        nc.sync.dma_start(out=v_hi[64:128, :].bitcast(I32), in_=v32[64:128, 0:256])
-        for Q in range(4):
-            nc.sync.dma_start(out=v_pl[32 * Q : 32 * Q + 4, :].bitcast(I32), in_=vs32[4 * Q : 4 * Q + 4, :])
+        nc.scalar.dma_start(out=v_pl[96:100, :].bitcast(I32), in_=vs32[12:16, :])
+        load_w(0, 0)
+        load_w(1, 0)
+        load_x(0, 2, 2)
         load_w(0, 1)
         load_w(1, 1)
         load_x(1, 0, 4)
-        nc.sync.dma_start(out=v_w[:].bitcast(I32), in_=v32[:, 256:512])
         load_x(2, 0, 4)
         load_x(3, 0, 4)
         nc.scalar.activation(out=junk[:, 0:1], in_=zero[:, 0:1], func=RELU)
 
-        warm = bank([128, 512], "y")
+        warm = bank([128, 512])
 
         def spin(n):
             for i in range(n):
                 nc.tensor.matmul(warm[:], lhsT=zero[:, 0:128], rhs=zero[:], start=True, stop=True)
 
-        spin(6)
+        spin(8)
 
         def permute_u(G):
             nc.vector.tensor_copy(
@@ -131,46 +126,26 @@ def tile_pointnet_set_encoder_s12_kernel(tc, x, w, u_words, u_scales, v_words, v
             c0 = G * 512 + t * 128
             return u_w[:, 2 * c0 : 2 * c0 + 256].bitcast(FP4X4), u_pl[:, c0 : c0 + 128]
 
-        def e0_mm(G, nq, tag):
-            if nq == 0:
-                e_grp[G, 0] = sb([128, 2048], BF16, "e_grp", 2)
-            e = bank([128, 4, 128], tag)
-            n = slice(nq * 128, nq * 128 + 128)
-            for t in range(4):
-                lhsT, lhsT_scale = u_tile(G, t)
-                for part, v in enumerate((v_lo, v_hi)):
-                    nc.tensor.matmul_mx(
-                        out=e[:, t, :], lhsT=lhsT, lhsT_scale=lhsT_scale,
-                        rhs=v[:, 2 * nq * 128 : 2 * nq * 128 + 256].bitcast(FP4X4), rhs_scale=v_pl[:, n],
-                        start=part == 0, stop=part == 1,
-                    )
-            e_bank[G, nq] = e
-
-        def e0_out(G, nq, engine):
-            copy(
-                engine,
-                e_grp[G, 0][:, 512 * nq : 512 * nq + 512].rearrange("p (n t) -> p n t", t=4),
-                e_bank[G, nq][:].rearrange("p t n -> p n t"),
-            )
-
-        def e1_mm(G, t, tag):
+        def e_mm(G, nh, t):
             if t == 0:
-                e_tmp[G] = sb([128, 4, 512], BF16, "e_tmp", 2)
-            e = bank([128, 512], tag)
+                e_tmp[G, nh] = sb([128, 4, 512], BF16, "e_tmp", 4)
+            e = bank([128, 512])
             lhsT, lhsT_scale = u_tile(G, t)
             nc.tensor.matmul_mx(
                 out=e[:], lhsT=lhsT, lhsT_scale=lhsT_scale,
-                rhs=v_w[:].bitcast(FP4X4), rhs_scale=v_pl[:, 512:1024], start=True, stop=True,
+                rhs=v_w[:, 1024 * nh : 1024 * nh + 1024].bitcast(FP4X4), rhs_scale=v_pl[:, 512 * nh : 512 * nh + 512],
+                start=True, stop=True,
             )
-            e_bank[G, 4 + t] = e
+            e_bank[G, nh, t] = e
 
-        def e1_out(G, t, engine):
-            copy(engine, e_tmp[G][:, t, :], e_bank[G, 4 + t][:])
+        def e_out(G, nh, t, engine):
+            copy(engine, e_tmp[G, nh][:, t, :], e_bank[G, nh, t][:])
 
-        def e1_weave(G):
-            e_grp[G, 1] = sb([128, 2048], BF16, "e_grp", 2)
-            nc.vector.tensor_copy(
-                out=e_grp[G, 1][:].rearrange("p (n t) -> p n t", t=4), in_=e_tmp[G][:].rearrange("p t n -> p n t")
+        def e_weave(G, nh, engine="V"):
+            e_grp[G, nh] = sb([128, 2048], BF16, "e_grp", 4)
+            copy(
+                engine,
+                e_grp[G, nh][:].rearrange("p (n t) -> p n t", t=4), e_tmp[G, nh][:].rearrange("p t n -> p n t"),
             )
 
         def e_quant(G, h):
@@ -191,12 +166,12 @@ def tile_pointnet_set_encoder_s12_kernel(tc, x, w, u_words, u_scales, v_words, v
                 in_=x_sb[c][:].bitcast(F32)[:, half].rearrange("p (a w u) -> p a u w", u=2, w=128),
             )
 
-        def x_transpose(c, bp, g, tag):
+        def x_transpose(c, bp, g):
             if (bp, g) == (0, 0):
                 x_g[c] = sb([128, 4096], BF16, "x_g", 2)
                 x_c[c] = sb([128, 1024], U32, "x_c", 2)
                 x_s[c] = sb([128, 1024], U8, "x_s", 2)
-            xt = bank([128, 2, 256], tag)
+            xt = bank([128, 2, 256])
             for u in range(2):
                 for bb in range(2):
                     base = (2 * bp + bb) * 512 + g * 256
@@ -225,7 +200,7 @@ def tile_pointnet_set_encoder_s12_kernel(tc, x, w, u_words, u_scales, v_words, v
         w_grp = {}
 
         def w_weave(g, G, engine, ts=(0, 1, 2, 3)):
-            if ts[0] == 0:
+            if (g, G) not in w_grp:
                 w_grp[g, G] = sb([128, 2048], BF16, "w_grp", 4)
             dst = w_grp[g, G][:].rearrange("p (t q r j) -> p t q r j", t=4, q=16, r=8, j=4)
             src = w_raw[g, G][:].rearrange("p j (q t r) -> p t q r j", q=16, t=4, r=8)
@@ -245,7 +220,7 @@ def tile_pointnet_set_encoder_s12_kernel(tc, x, w, u_words, u_scales, v_words, v
             G, b = i // 4, i % 4
             if b == 0:
                 h_t[c, G] = sb([128, 2048], BF16, "h_t", 3)
-            h = bank([128, 4, 128], "h")
+            h = bank([128, 4, 128])
             col = (b // 2) * 512 + (b % 2) * 128
             for t in range(4):
                 for g in range(2):
@@ -257,16 +232,22 @@ def tile_pointnet_set_encoder_s12_kernel(tc, x, w, u_words, u_scales, v_words, v
                         rhs=x_c[c][:, k].bitcast(FP8X4), rhs_scale=x_s[c][:, k],
                         start=g == 0, stop=g == 1,
                     )
-            nc.scalar.activation(
-                out=h_t[c, G][:, 512 * b : 512 * b + 512].rearrange("p (n t) -> p n t", t=4),
-                in_=h[:].rearrange("p t n -> p n t"), func=RELU,
-            )
+            h_bank[c, i] = h
+
+        def h_out(c, i, engine="S"):
+            G, b = i // 4, i % 4
+            dst = h_t[c, G][:, 512 * b : 512 * b + 512].rearrange("p (n t) -> p n t", t=4)
+            src = h_bank[c, i][:].rearrange("p t n -> p n t")
+            if engine == "S":
+                nc.scalar.activation(out=dst, in_=src, func=RELU)
+            else:
+                nc.vector.tensor_scalar_max(dst, src, 0.0)
 
         def h_quant(c, G):
             nc.vector.quantize_mx(out=h_c[c, G][:].bitcast(FP8X4), scales=h_s[c, G][:], in_=h_t[c, G][:])
 
         def mm2(c, b, nh):
-            y = bank([128, 512], "y")
+            y = bank([128, 512])
             rows = slice(128 * b, 128 * b + 128)
             for G in range(2):
                 nc.tensor.matmul_mx(
@@ -284,93 +265,80 @@ def tile_pointnet_set_encoder_s12_kernel(tc, x, w, u_words, u_scales, v_words, v
                 s = c // 2
                 nc.sync.dma_start(out=out[128 * s : 128 * s + 128, 512 * nh : 512 * nh + 512], in_=a)
 
-        w_weave(0, 0, "S", (0, 1))
-        w_weave(0, 0, "V", (2, 3))
-        for g in range(2):
-            x_transpose(0, 0, g, "tr")
-            x_out(0, 0, g, "S")
-        spin(2)
-        w_quant(0, 0)
-        w_weave(1, 0, "V")
-        w_quant(1, 0)
-        x_quant(0, 0)
-        for g in range(2):
-            x_transpose(0, 1, g, "h")
-            x_out(0, 1, g, "S")
-        spin(2)
-        x_quant(0, 1)
-
-        mm1(0, 0)
         permute_u(0)
         permute_u_scales(0)
-        mm1(0, 1)
-        permute_u(1)
         permute_u_scales(1)
-        mm1(0, 2)
-        mm1(0, 3)
-        w_weave(0, 1, "V")
-        for nq in range(4):
-            e0_mm(0, nq, "y" if nq < 2 else "tr")
-            e0_out(0, nq, "S")
-        w_quant(0, 1)
-        w_weave(1, 1, "V")
-        w_quant(1, 1)
-        for g in range(2):
-            x_transpose(1, 0, g, "tr")
-            x_out(1, 0, g, "S")
-        for nq in range(4):
-            e0_mm(1, nq, "y")
-            e0_out(1, nq, "VS"[nq % 2])
-        h_quant(0, 0)
-        mm1(0, 4)
-        x_quant(1, 0)
-        e_quant(0, 0)
-        mm1(0, 5)
-        for g in range(2):
-            x_transpose(1, 1, g, "tr")
-            x_out(1, 1, g, "V")
-        mm1(0, 6)
-        e_quant(1, 0)
-        x_quant(1, 1)
-        mm1(0, 7)
+        permute_u(1)
+        x_transpose(0, 0, 0)
+        x_transpose(0, 0, 1)
+        x_out(0, 0, 0, "S")
+        x_out(0, 0, 1, "V")
+        spin(2)
+        for t in range(4):
+            e_mm(0, 0, t)
+            e_out(0, 0, t, "SV"[t % 2])
+        x_quant(0, 0)
+        w_weave(0, 0, "S", (0, 1))
+        w_weave(0, 0, "V", (2, 3))
+        e_mm(1, 0, 0)
+        e_mm(1, 0, 1)
+        e_mm(1, 0, 2)
+        e_mm(1, 0, 3)
+        w_weave(1, 0, "V", (2, 3))
+        w_weave(1, 0, "S", (0, 1))
+        w_quant(0, 0)
+        e_out(1, 0, 0, "V")
+        w_quant(1, 0)
+        e_out(1, 0, 1, "S")
+        e_out(1, 0, 2, "V")
+        e_out(1, 0, 3, "S")
+        x_transpose(0, 1, 0)
+        x_transpose(0, 1, 1)
+        x_out(0, 1, 0, "S")
+        x_out(0, 1, 1, "V")
+        x_quant(0, 1)
 
-        second = [(0, b, 0) for b in range(4)] + [(0, b, 1) for b in range(4)]
-        second += [(c, b, nh) for c in (1, 2, 3) for b in range(4) for nh in range(2)]
-        e1_slots = {0: (0, (0, 1)), 1: (0, (2, 3)), 4: (1, (0, 1)), 5: (1, (2, 3))}
-        done = 0
-        for c in (1, 2, 3):
+        for c in range(4):
             for i in range(8):
                 mm1(c, i)
-                if i == 1:
-                    h_quant(c - 1, 1)
-                if i == 4 and c < 3:
-                    x_quant(c + 1, 0)
-                if i == 5:
+                h_out(c, i)
+                if c == 0:
+                    if i == 0:
+                        w_weave(0, 1, "S", (0, 1))
+                        w_weave(0, 1, "V", (2, 3))
+                        w_weave(1, 1, "V", (2, 3))
+                    if i == 1:
+                        w_quant(0, 1)
+                        w_weave(1, 1, "S", (0, 1))
+                    if i == 2:
+                        w_quant(1, 1)
+                    if i >= 4:
+                        G, t = i // 2 - 2, 2 * (i % 2)
+                        e_mm(G, 1, t)
+                        e_mm(G, 1, t + 1)
+                        e_out(G, 1, t, "V")
+                        e_out(G, 1, t + 1, "S")
+                if c < 3 and i in (1, 3):
+                    for g in range(2):
+                        x_transpose(c + 1, i // 2, g)
+                        x_out(c + 1, i // 2, g, "VS"[g])
+                if c < 3 and i in (4, 5):
+                    x_quant(c + 1, i - 4)
+                if i == 6:
                     h_quant(c, 0)
-                if i == 7 and c < 3:
-                    x_quant(c + 1, 1)
-                if c < 3 and i in (0, 3):
-                    x_reorder(c + 1, i // 3)
-                if c == 1 and i in e1_slots:
-                    G, ts = e1_slots[i]
-                    for t in ts:
-                        e1_mm(G, t, "y")
-                        e1_out(G, t, "SV"[t % 2])
-                    if ts[1] == 3:
-                        e1_weave(G)
-                else:
-                    mm2(*second[done])
-                    done += 1
-                if c == 1 and i == 3:
-                    e_quant(0, 1)
-                if c == 1 and i == 7:
-                    e_quant(1, 1)
-                if c < 3 and i in (2, 5):
-                    bp = i // 3
-                    for g in range(2):
-                        x_transpose(c + 1, bp, g, "tr")
-                    for g in range(2):
-                        x_out(c + 1, bp, g, "S")
+                if c > 0 and i == 1:
+                    h_quant(c - 1, 1)
+                if c == 0 and i >= 6 or c == 1 and i in (0, 2):
+                    x_reorder(2 + c, i % 4 // 2 if c else i - 6)
+                if c == 1 and i in (5, 7) or c == 2 and i in (1, 3):
+                    k = i // 2 - 2 if c == 1 else i // 2 + 2
+                    e_weave(k % 2, k // 2)
+                if c == 3 and i % 2 == 0:
+                    k = i // 2
+                    e_quant(k % 2, k // 2)
         h_quant(3, 1)
-        for item in second[done:]:
-            mm2(*item)
+
+        for c in range(4):
+            for b in range(4):
+                for nh in range(2):
+                    mm2(c, b, nh)

@@ -15,7 +15,7 @@ FP4X4 = mybir.dt.float4_e2m1fn_x4
 MAX = mybir.AluOpType.max
 RELU = mybir.ActivationFunctionType.Relu
 
-REORDERED = (2, 3)
+REORDERED = (1, 2, 3)
 
 
 def tile_pointnet_set_encoder_s12_kernel(tc, x, w, u_words, u_scales, v_words, v_scales, out):
@@ -52,9 +52,9 @@ def tile_pointnet_set_encoder_s12_kernel(tc, x, w, u_words, u_scales, v_words, v
         h_s = {(c, G): sb([128, 512], U8, "h_s%d%d" % (c, G)) for c in range(4) for G in range(2)}
         acc = [sb([128, 1024], F32, "acc%d" % s) for s in range(2)]
 
-        nc.vector.memset(zero[:], 0.0)
         nc.vector.memset(u_pl_raw[:].bitcast(I32), 0)
         nc.vector.memset(v_pl[:].bitcast(I32), 0)
+        nc.vector.memset(zero[:], 0.0)
 
         v32 = v_words[0].bitcast(I32)
         us32 = u_scales[0].bitcast(I32)
@@ -73,23 +73,23 @@ def tile_pointnet_set_encoder_s12_kernel(tc, x, w, u_words, u_scales, v_words, v
         def load_w(g, G):
             nc.sync.dma_start(out=w_raw[g, G][:], in_=wv[g][:, :, 512 * G : 512 * G + 512])
 
-        make_identity(nc, ident[:])
+        for Q in range(4):
+            nc.scalar.dma_start(out=u_pl_raw[32 * Q : 32 * Q + 4, :].bitcast(I32), in_=us32[4 * Q : 4 * Q + 4, :])
         for Q in range(3):
             nc.gpsimd.dma_start(out=v_pl[32 * Q : 32 * Q + 4, :].bitcast(I32), in_=vs32[4 * Q : 4 * Q + 4, :])
+        make_identity(nc, ident[:])
+        load_w(0, 0)
         load_x(0, 0, 2)
         nc.sync.dma_start(out=u_raw[:].bitcast(I32), in_=u_words[0].bitcast(I32))
         nc.sync.dma_start(out=v_w[:].bitcast(I32), in_=v32)
-        for Q in range(4):
-            nc.scalar.dma_start(out=u_pl_raw[32 * Q : 32 * Q + 4, :].bitcast(I32), in_=us32[4 * Q : 4 * Q + 4, :])
-        nc.scalar.dma_start(out=v_pl[96:100, :].bitcast(I32), in_=vs32[12:16, :])
-        load_w(0, 0)
+        nc.sync.dma_start(out=v_pl[96:100, :].bitcast(I32), in_=vs32[12:16, :])
         load_w(1, 0)
         load_x(0, 2, 2)
         load_w(0, 1)
         load_w(1, 1)
-        load_x(1, 0, 4)
-        load_x(2, 0, 4)
-        load_x(3, 0, 4)
+        for c in (1, 2, 3):
+            for b0 in (0, 2):
+                load_x(c, b0, 2)
         nc.scalar.activation(out=junk[:, 0:1], in_=zero[:, 0:1], func=RELU)
 
         warm = bank([128, 512])
@@ -159,7 +159,7 @@ def tile_pointnet_set_encoder_s12_kernel(tc, x, w, u_words, u_scales, v_words, v
 
         def x_reorder(c, bp):
             if bp == 0:
-                x_r[c] = sb([128, 4096], BF16, "x_r", 2)
+                x_r[c] = sb([128, 4096], BF16, "x_r", 3)
             half = slice(1024 * bp, 1024 * bp + 1024)
             nc.vector.tensor_copy(
                 out=x_r[c][:].bitcast(F32)[:, half].rearrange("p (a u w) -> p a u w", u=2, w=128),
@@ -246,25 +246,29 @@ def tile_pointnet_set_encoder_s12_kernel(tc, x, w, u_words, u_scales, v_words, v
         def h_quant(c, G):
             nc.vector.quantize_mx(out=h_c[c, G][:].bitcast(FP8X4), scales=h_s[c, G][:], in_=h_t[c, G][:])
 
-        def mm2(c, b, nh):
-            y = bank([128, 512])
+        def mm2(c, b, n0, n):
+            y = bank([128, n])
             rows = slice(128 * b, 128 * b + 128)
+            nh, j0 = n0 // 512, n0 % 512
             for G in range(2):
                 nc.tensor.matmul_mx(
                     out=y[:],
                     lhsT=h_c[c, G][:, rows].bitcast(FP8X4), lhsT_scale=h_s[c, G][:, rows],
-                    rhs=e_c[G, nh][:].bitcast(FP8X4), rhs_scale=e_s[G, nh][:],
+                    rhs=e_c[G, nh][:, j0 : j0 + n].bitcast(FP8X4), rhs_scale=e_s[G, nh][:, j0 : j0 + n],
                     start=G == 0, stop=G == 1,
                 )
-            a = acc[c // 2][:, 512 * nh : 512 * nh + 512]
+            a = acc[c // 2][:, n0 : n0 + n]
             if c % 2 == 0 and b == 0:
                 nc.scalar.activation(out=a, in_=y[:], func=RELU)
             else:
                 nc.vector.tensor_tensor(out=a, in0=y[:], in1=a, op=MAX)
             if c % 2 == 1 and b == 3:
                 s = c // 2
-                nc.sync.dma_start(out=out[128 * s : 128 * s + 128, 512 * nh : 512 * nh + 512], in_=a)
+                nc.sync.dma_start(out=out[128 * s : 128 * s + 128, n0 : n0 + n], in_=a)
 
+        e_units = [(G, nh, t) for nh in range(2) for G in range(2) for t in range(4)]
+        w_weave(0, 0, "S", (0, 1))
+        w_weave(0, 0, "V", (2, 3))
         permute_u(0)
         permute_u_scales(0)
         permute_u_scales(1)
@@ -272,31 +276,26 @@ def tile_pointnet_set_encoder_s12_kernel(tc, x, w, u_words, u_scales, v_words, v
         x_transpose(0, 0, 0)
         x_transpose(0, 0, 1)
         x_out(0, 0, 0, "S")
-        x_out(0, 0, 1, "V")
-        spin(2)
-        for t in range(4):
-            e_mm(0, 0, t)
-            e_out(0, 0, t, "SV"[t % 2])
-        x_quant(0, 0)
-        w_weave(0, 0, "S", (0, 1))
-        w_weave(0, 0, "V", (2, 3))
-        e_mm(1, 0, 0)
-        e_mm(1, 0, 1)
-        e_mm(1, 0, 2)
-        e_mm(1, 0, 3)
-        w_weave(1, 0, "V", (2, 3))
-        w_weave(1, 0, "S", (0, 1))
+        x_out(0, 0, 1, "S")
         w_quant(0, 0)
-        e_out(1, 0, 0, "V")
+        for k in range(8):
+            e_mm(*e_units[k])
+        for k in range(5):
+            e_out(*e_units[k], "S")
+        w_weave(1, 0, "V")
+        x_quant(0, 0)
         w_quant(1, 0)
-        e_out(1, 0, 1, "S")
-        e_out(1, 0, 2, "V")
-        e_out(1, 0, 3, "S")
+        for k in range(8, 12):
+            e_mm(*e_units[k])
         x_transpose(0, 1, 0)
         x_transpose(0, 1, 1)
+        e_out(*e_units[5], "V")
+        e_out(*e_units[6], "S")
         x_out(0, 1, 0, "S")
         x_out(0, 1, 1, "V")
         x_quant(0, 1)
+        for k in range(7, 12):
+            e_out(*e_units[k], "S")
 
         for c in range(4):
             for i in range(8):
@@ -304,24 +303,28 @@ def tile_pointnet_set_encoder_s12_kernel(tc, x, w, u_words, u_scales, v_words, v
                 h_out(c, i)
                 if c == 0:
                     if i == 0:
-                        w_weave(0, 1, "S", (0, 1))
-                        w_weave(0, 1, "V", (2, 3))
-                        w_weave(1, 1, "V", (2, 3))
+                        x_reorder(1, 0)
+                        w_weave(0, 1, "V", (1, 2, 3))
+                        w_weave(0, 1, "S", (0,))
                     if i == 1:
+                        x_reorder(1, 1)
+                        w_weave(1, 1, "V", (1, 2, 3))
                         w_quant(0, 1)
-                        w_weave(1, 1, "S", (0, 1))
-                    if i == 2:
+                        w_weave(1, 1, "S", (0,))
                         w_quant(1, 1)
-                    if i >= 4:
-                        G, t = i // 2 - 2, 2 * (i % 2)
-                        e_mm(G, 1, t)
-                        e_mm(G, 1, t + 1)
-                        e_out(G, 1, t, "V")
-                        e_out(G, 1, t + 1, "S")
-                if c < 3 and i in (1, 3):
-                    for g in range(2):
-                        x_transpose(c + 1, i // 2, g)
-                        x_out(c + 1, i // 2, g, "VS"[g])
+                    if i == 3:
+                        for bp in range(2):
+                            for g in range(2):
+                                x_transpose(1, bp, g)
+                                x_out(1, bp, g, "VS"[g])
+                        for k in range(12, 16):
+                            e_mm(*e_units[k])
+                            e_out(*e_units[k], "VS"[k % 2])
+                if c in (1, 2) and i == 2:
+                    for bp in range(2):
+                        for g in range(2):
+                            x_transpose(c + 1, bp, g)
+                            x_out(c + 1, bp, g, "VS"[g])
                 if c < 3 and i in (4, 5):
                     x_quant(c + 1, i - 4)
                 if i == 6:
@@ -330,9 +333,8 @@ def tile_pointnet_set_encoder_s12_kernel(tc, x, w, u_words, u_scales, v_words, v
                     h_quant(c - 1, 1)
                 if c == 0 and i >= 6 or c == 1 and i in (0, 2):
                     x_reorder(2 + c, i % 4 // 2 if c else i - 6)
-                if c == 1 and i in (5, 7) or c == 2 and i in (1, 3):
-                    k = i // 2 - 2 if c == 1 else i // 2 + 2
-                    e_weave(k % 2, k // 2)
+                if c in (1, 2) and i in (5, 7):
+                    e_weave(i // 2 - 2, c - 1)
                 if c == 3 and i % 2 == 0:
                     k = i // 2
                     e_quant(k % 2, k // 2)
@@ -340,5 +342,6 @@ def tile_pointnet_set_encoder_s12_kernel(tc, x, w, u_words, u_scales, v_words, v
 
         for c in range(4):
             for b in range(4):
-                for nh in range(2):
-                    mm2(c, b, nh)
+                widths = (512, 256, 256) if (c, b) == (3, 3) else (512, 512)
+                for j, n in enumerate(widths):
+                    mm2(c, b, sum(widths[:j]), n)

from contextlib import ExitStack

import concourse.mybir as mybir
from concourse.masks import make_identity

FLOPS = 2 * 2048 * 1024 * 1024 * 2 + 2 * 512 * 1024 * 1024

F32 = mybir.dt.float32
BF16 = mybir.dt.bfloat16
I32 = mybir.dt.int32
U32 = mybir.dt.uint32
U8 = mybir.dt.uint8
FP8X4 = mybir.dt.float8_e4m3fn_x4
FP4X4 = mybir.dt.float4_e2m1fn_x4
MAX = mybir.AluOpType.max
RELU = mybir.ActivationFunctionType.Relu

REORDERED = (1, 2, 3)


def tile_pointnet_set_encoder_s12_kernel(tc, x, w, u_words, u_scales, v_words, v_scales, out):
    nc = tc.nc
    with ExitStack() as ctx:
        keep = ctx.enter_context(tc.tile_pool(name="keep", bufs=1))
        psum = ctx.enter_context(tc.psum_pool(name="psum", bufs=1))
        ctx.enter_context(tc.manual_schedule())

        def sb(shape, dtype, tag, bufs=1):
            t = keep.tile(shape, dtype, name=tag, tag=tag, bufs=bufs, align_bytes=256)
            return t

        def bank(shape):
            t = psum.tile(shape, F32, name="bank", tag="bank", bufs=8)
            return t

        u_raw = sb([128, 2048], U8, "u_raw")
        u_w = sb([128, 2048], U8, "u_w")
        u_pl_raw = sb([128, 1024], U8, "u_pl_raw")
        u_pl = sb([128, 1024], U8, "u_pl")
        v_w = sb([128, 2048], U8, "v_w")
        v_pl = sb([128, 1024], U8, "v_pl")
        ident = sb([128, 128], F32, "ident")
        zero = sb([128, 512], BF16, "zero")
        junk = sb([128, 16], BF16, "junk")
        x_sb = [sb([128, 4096], BF16, "x_sb%d" % c) for c in range(4)]
        w_raw = {(g, G): sb([128, 4, 512], BF16, "w_raw%d%d" % (g, G)) for G in range(2) for g in range(2)}
        w_c = {(g, G): sb([128, 512], U32, "w_c%d%d" % (g, G)) for G in range(2) for g in range(2)}
        w_s = {(g, G): sb([128, 512], U8, "w_s%d%d" % (g, G)) for G in range(2) for g in range(2)}
        e_c = {(G, h): sb([128, 512], U32, "e_c%d%d" % (G, h)) for G in range(2) for h in range(2)}
        e_s = {(G, h): sb([128, 512], U8, "e_s%d%d" % (G, h)) for G in range(2) for h in range(2)}
        h_c = {(c, G): sb([128, 512], U32, "h_c%d%d" % (c, G)) for c in range(4) for G in range(2)}
        h_s = {(c, G): sb([128, 512], U8, "h_s%d%d" % (c, G)) for c in range(4) for G in range(2)}
        acc = [sb([128, 1024], F32, "acc%d" % s) for s in range(2)]

        nc.vector.memset(u_pl_raw[:].bitcast(I32), 0)
        nc.vector.memset(v_pl[:].bitcast(I32), 0)
        nc.vector.memset(zero[:], 0.0)

        v32 = v_words[0].bitcast(I32)
        us32 = u_scales[0].bitcast(I32)
        vs32 = v_scales[0].bitcast(I32)

        xv = x.rearrange("(s i b) k -> s i b k", s=2, i=128, b=8)
        wv = w.rearrange("(g p j) f -> g p j f", g=2, p=128, j=4)

        def load_x(c, b0, nb):
            s, base = c // 2, 4 * (c % 2)
            nc.sync.dma_start(
                out=x_sb[c][:].rearrange("p (b k) -> p b k", b=4)[:, b0 : b0 + nb, :],
                in_=xv[s][:, base + b0 : base + b0 + nb, :],
            )

        def load_w(g, G):
            nc.sync.dma_start(out=w_raw[g, G][:], in_=wv[g][:, :, 512 * G : 512 * G + 512])

        for Q in range(4):
            nc.scalar.dma_start(out=u_pl_raw[32 * Q : 32 * Q + 4, :].bitcast(I32), in_=us32[4 * Q : 4 * Q + 4, :])
        for Q in range(3):
            nc.gpsimd.dma_start(out=v_pl[32 * Q : 32 * Q + 4, :].bitcast(I32), in_=vs32[4 * Q : 4 * Q + 4, :])
        make_identity(nc, ident[:])
        load_w(0, 0)
        load_x(0, 0, 2)
        nc.sync.dma_start(out=u_raw[:].bitcast(I32), in_=u_words[0].bitcast(I32))
        nc.sync.dma_start(out=v_w[:].bitcast(I32), in_=v32)
        nc.sync.dma_start(out=v_pl[96:100, :].bitcast(I32), in_=vs32[12:16, :])
        load_w(1, 0)
        load_x(0, 2, 2)
        load_w(0, 1)
        load_w(1, 1)
        for c in (1, 2, 3):
            for b0 in (0, 2):
                load_x(c, b0, 2)
        nc.scalar.activation(out=junk[:, 0:1], in_=zero[:, 0:1], func=RELU)

        warm = bank([128, 512])

        def spin(n):
            for i in range(n):
                nc.tensor.matmul(warm[:], lhsT=zero[:, 0:128], rhs=zero[:], start=True, stop=True)

        spin(8)

        def permute_u(G):
            nc.vector.tensor_copy(
                out=u_w[:].bitcast(I32).rearrange("p (G t q r) -> p G t q r", G=2, t=4, q=16, r=4)[:, G],
                in_=u_raw[:].bitcast(I32).rearrange("p (G q t r) -> p G t q r", G=2, q=16, t=4, r=4)[:, G],
            )

        def permute_u_scales(G):
            nc.vector.tensor_copy(
                out=u_pl[:].bitcast(I32).rearrange("p (G t q r) -> p G t q r", G=2, t=4, q=16, r=2)[:, G],
                in_=u_pl_raw[:].bitcast(I32).rearrange("p (G q t r) -> p G t q r", G=2, q=16, t=4, r=2)[:, G],
            )

        def copy(engine, out, in_):
            if engine == "S":
                nc.scalar.copy(out, in_)
            else:
                nc.vector.tensor_copy(out=out, in_=in_)

        e_grp = {}
        e_tmp = {}
        e_bank = {}

        def u_tile(G, t):
            c0 = G * 512 + t * 128
            return u_w[:, 2 * c0 : 2 * c0 + 256].bitcast(FP4X4), u_pl[:, c0 : c0 + 128]

        def e_mm(G, nh, t):
            if t == 0:
                e_tmp[G, nh] = sb([128, 4, 512], BF16, "e_tmp", 4)
            e = bank([128, 512])
            lhsT, lhsT_scale = u_tile(G, t)
            nc.tensor.matmul_mx(
                out=e[:], lhsT=lhsT, lhsT_scale=lhsT_scale,
                rhs=v_w[:, 1024 * nh : 1024 * nh + 1024].bitcast(FP4X4), rhs_scale=v_pl[:, 512 * nh : 512 * nh + 512],
                start=True, stop=True,
            )
            e_bank[G, nh, t] = e

        def e_out(G, nh, t, engine):
            copy(engine, e_tmp[G, nh][:, t, :], e_bank[G, nh, t][:])

        def e_weave(G, nh, engine="V"):
            e_grp[G, nh] = sb([128, 2048], BF16, "e_grp", 4)
            copy(
                engine,
                e_grp[G, nh][:].rearrange("p (n t) -> p n t", t=4), e_tmp[G, nh][:].rearrange("p t n -> p n t"),
            )

        def e_quant(G, h):
            nc.vector.quantize_mx(out=e_c[G, h][:].bitcast(FP8X4), scales=e_s[G, h][:], in_=e_grp[G, h][:])

        x_r = {}
        x_g = {}
        x_c = {}
        x_s = {}
        x_bank = {}

        def x_reorder(c, bp):
            if bp == 0:
                x_r[c] = sb([128, 4096], BF16, "x_r", 3)
            half = slice(1024 * bp, 1024 * bp + 1024)
            nc.vector.tensor_copy(
                out=x_r[c][:].bitcast(F32)[:, half].rearrange("p (a u w) -> p a u w", u=2, w=128),
                in_=x_sb[c][:].bitcast(F32)[:, half].rearrange("p (a w u) -> p a u w", u=2, w=128),
            )

        def x_transpose(c, bp, g):
            if (bp, g) == (0, 0):
                x_g[c] = sb([128, 4096], BF16, "x_g", 2)
                x_c[c] = sb([128, 1024], U32, "x_c", 2)
                x_s[c] = sb([128, 1024], U8, "x_s", 2)
            xt = bank([128, 2, 256])
            for u in range(2):
                for bb in range(2):
                    base = (2 * bp + bb) * 512 + g * 256
                    if c in REORDERED:
                        words = x_r[c][:].bitcast(F32)[:, base + 128 * u : base + 128 * u + 128]
                    else:
                        words = x_sb[c][:].bitcast(F32)[:, base + u : base + 256 : 2]
                    nc.tensor.transpose(xt[:, u, 128 * bb : 128 * bb + 128], words, ident[:])
            x_bank[c, bp, g] = xt

        def x_out(c, bp, g, engine):
            base = (2 * bp + g) * 1024
            copy(
                engine,
                x_g[c][:, base : base + 1024].bitcast(F32).rearrange("p (n u) -> p n u", u=2),
                x_bank[c, bp, g][:].rearrange("p u n -> p n u"),
            )

        def x_quant(c, bp):
            nc.vector.quantize_mx(
                out=x_c[c][:, 512 * bp : 512 * bp + 512].bitcast(FP8X4),
                scales=x_s[c][:, 512 * bp : 512 * bp + 512],
                in_=x_g[c][:, 2048 * bp : 2048 * bp + 2048],
            )

        w_grp = {}

        def w_weave(g, G, engine, ts=(0, 1, 2, 3)):
            if (g, G) not in w_grp:
                w_grp[g, G] = sb([128, 2048], BF16, "w_grp", 4)
            dst = w_grp[g, G][:].rearrange("p (t q r j) -> p t q r j", t=4, q=16, r=8, j=4)
            src = w_raw[g, G][:].rearrange("p j (q t r) -> p t q r j", q=16, t=4, r=8)
            if engine == "V":
                nc.vector.tensor_copy(out=dst[:, ts[0] : ts[-1] + 1], in_=src[:, ts[0] : ts[-1] + 1])
            else:
                for t in ts:
                    nc.scalar.copy(dst[:, t], src[:, t])

        def w_quant(g, G):
            nc.vector.quantize_mx(out=w_c[g, G][:].bitcast(FP8X4), scales=w_s[g, G][:], in_=w_grp[g, G][:])

        h_t = {}
        h_bank = {}

        def mm1(c, i):
            G, b = i // 4, i % 4
            if b == 0:
                h_t[c, G] = sb([128, 2048], BF16, "h_t", 3)
            h = bank([128, 4, 128])
            col = (b // 2) * 512 + (b % 2) * 128
            for t in range(4):
                for g in range(2):
                    k = slice(col + 256 * g, col + 256 * g + 128)
                    nc.tensor.matmul_mx(
                        out=h[:, t, :],
                        lhsT=w_c[g, G][:, 128 * t : 128 * t + 128].bitcast(FP8X4),
                        lhsT_scale=w_s[g, G][:, 128 * t : 128 * t + 128],
                        rhs=x_c[c][:, k].bitcast(FP8X4), rhs_scale=x_s[c][:, k],
                        start=g == 0, stop=g == 1,
                    )
            h_bank[c, i] = h

        def h_out(c, i, engine="S"):
            G, b = i // 4, i % 4
            dst = h_t[c, G][:, 512 * b : 512 * b + 512].rearrange("p (n t) -> p n t", t=4)
            src = h_bank[c, i][:].rearrange("p t n -> p n t")
            if engine == "S":
                nc.scalar.activation(out=dst, in_=src, func=RELU)
            else:
                nc.vector.tensor_scalar_max(dst, src, 0.0)

        def h_quant(c, G):
            nc.vector.quantize_mx(out=h_c[c, G][:].bitcast(FP8X4), scales=h_s[c, G][:], in_=h_t[c, G][:])

        def mm2(c, b, n0, n):
            y = bank([128, n])
            rows = slice(128 * b, 128 * b + 128)
            nh, j0 = n0 // 512, n0 % 512
            for G in range(2):
                nc.tensor.matmul_mx(
                    out=y[:],
                    lhsT=h_c[c, G][:, rows].bitcast(FP8X4), lhsT_scale=h_s[c, G][:, rows],
                    rhs=e_c[G, nh][:, j0 : j0 + n].bitcast(FP8X4), rhs_scale=e_s[G, nh][:, j0 : j0 + n],
                    start=G == 0, stop=G == 1,
                )
            a = acc[c // 2][:, n0 : n0 + n]
            if c % 2 == 0 and b == 0:
                nc.scalar.activation(out=a, in_=y[:], func=RELU)
            else:
                nc.vector.tensor_tensor(out=a, in0=y[:], in1=a, op=MAX)
            if c % 2 == 1 and b == 3:
                s = c // 2
                nc.sync.dma_start(out=out[128 * s : 128 * s + 128, n0 : n0 + n], in_=a)

        e_units = [(G, nh, t) for nh in range(2) for G in range(2) for t in range(4)]
        w_weave(0, 0, "S", (0, 1))
        w_weave(0, 0, "V", (2, 3))
        permute_u(0)
        permute_u_scales(0)
        permute_u_scales(1)
        permute_u(1)
        x_transpose(0, 0, 0)
        x_transpose(0, 0, 1)
        x_out(0, 0, 0, "S")
        x_out(0, 0, 1, "S")
        w_quant(0, 0)
        for k in range(8):
            e_mm(*e_units[k])
        for k in range(5):
            e_out(*e_units[k], "S")
        w_weave(1, 0, "V")
        x_quant(0, 0)
        w_quant(1, 0)
        for k in range(8, 12):
            e_mm(*e_units[k])
        x_transpose(0, 1, 0)
        x_transpose(0, 1, 1)
        e_out(*e_units[5], "V")
        e_out(*e_units[6], "S")
        x_out(0, 1, 0, "S")
        x_out(0, 1, 1, "V")
        x_quant(0, 1)
        for k in range(7, 12):
            e_out(*e_units[k], "S")

        for c in range(4):
            for i in range(8):
                mm1(c, i)
                h_out(c, i)
                if c == 0:
                    if i == 0:
                        x_reorder(1, 0)
                        w_weave(0, 1, "V", (1, 2, 3))
                        w_weave(0, 1, "S", (0,))
                    if i == 1:
                        x_reorder(1, 1)
                        w_weave(1, 1, "V", (1, 2, 3))
                        w_quant(0, 1)
                        w_weave(1, 1, "S", (0,))
                        w_quant(1, 1)
                    if i == 3:
                        for bp in range(2):
                            for g in range(2):
                                x_transpose(1, bp, g)
                                x_out(1, bp, g, "VS"[g])
                        for k in range(12, 16):
                            e_mm(*e_units[k])
                            e_out(*e_units[k], "VS"[k % 2])
                if c in (1, 2) and i == 2:
                    for bp in range(2):
                        for g in range(2):
                            x_transpose(c + 1, bp, g)
                            x_out(c + 1, bp, g, "VS"[g])
                if c < 3 and i in (4, 5):
                    x_quant(c + 1, i - 4)
                if i == 6:
                    h_quant(c, 0)
                if c > 0 and i == 1:
                    h_quant(c - 1, 1)
                if c == 0 and i >= 6 or c == 1 and i in (0, 2):
                    x_reorder(2 + c, i % 4 // 2 if c else i - 6)
                if c in (1, 2) and i in (5, 7):
                    e_weave(i // 2 - 2, c - 1)
                if c == 3 and i % 2 == 0:
                    k = i // 2
                    e_quant(k % 2, k // 2)
        h_quant(3, 1)

        for c in range(4):
            for b in range(4):
                widths = (512, 256, 256) if (c, b) == (3, 3) else (512, 512)
                for j, n in enumerate(widths):
                    mm2(c, b, sum(widths[:j]), n)
